import numpy as np
import ml_dtypes


def mxq(x, axis, fmt="e4m3"):
    dtype, down = {"e4m3": (ml_dtypes.float8_e4m3fn, 7), "e5m2": (ml_dtypes.float8_e5m2, 14)}[fmt]
    v = np.moveaxis(np.asarray(x, np.float32).astype(ml_dtypes.bfloat16).astype(np.float64), axis, -1)
    blocks = v.reshape(v.shape[:-1] + (-1, 32))
    amax = np.abs(blocks).max(-1, keepdims=True)
    byte = np.maximum(np.where(amax > 0, np.frexp(amax)[1] - 1 + 127, 0) - down, 1)
    scale = np.exp2(byte - 127.0)
    codes = (blocks / scale).astype(np.float32).astype(dtype).astype(np.float64)
    return np.moveaxis((codes * scale).reshape(v.shape), -1, axis)


WIDE = False


def mx_kscale(k):
    if not WIDE:
        return np.ones(k)
    levels = np.array([10, -10, 5, -5, 0])
    if k % 512:
        return np.exp2(np.random.permutation(np.resize(levels, k // 32))).repeat(32)
    a = np.empty((k // 512, 16))
    for p in range(k // 512):
        a[p, :8] = np.random.permutation(np.resize(levels, 8))
        for g in range(8):
            far = levels[np.abs(levels - a[p, g]) >= 10]
            a[p, g + 8] = far[np.random.randint(len(far))]
    return np.exp2(a.ravel()).repeat(32)


def f64(x):
    return np.asarray(x).astype(np.float64)


def striped(idx):
    return np.tile(idx.reshape(-1, 16).T, (8, 1)).astype(np.uint16)


def unstriped(offs):
    return offs[:16].T.reshape(-1).astype(np.int64)


K, T, E, C, N = 2560, 768, 4, 128, 512
M = 512


def by_expert(wq, xq):
    return np.concatenate([wq[e].T @ xq[:, e * C:(e + 1) * C] for e in range(E)], axis=1)


def setup_inputs():
    n = np.random.standard_normal
    s = mx_kscale(K)[:, None]
    v = mx_kscale(N)
    return {
        "xT": (n((K, T)) * s).astype(np.float32),
        "w": (n((E, K, N)) / np.sqrt(K) / s[None] * v[None, None, :]).astype(np.float32),
        "b": (0.3 * n((N, E)) * v[:, None]).astype(np.float32),
        "wp": (n((N, M)) / np.sqrt(N) / v[:, None]).astype(np.float32),
        "gate": np.tile(np.random.uniform(0.2, 1.0, E * C), (N, 1)).astype(np.float32),
        "offs": striped(np.random.permutation(T)[:E * C]),
    }


def reference(xT, w, b, wp, gate, offs):
    idx = unstriped(offs)
    xq = mxq(f64(xT)[:, idx], 0, "e4m3")
    y = by_expert(mxq(f64(w), 1, "e4m3"), xq)
    y = y + np.repeat(f64(b), C, axis=1)
    c = np.zeros((N, T))
    c[:, idx] = f64(gate) * y
    return mxq(f64(wp), 0, "e4m3").T @ mxq(c, 0, "e4m3")

@@ -1,0 +1,251 @@
+from contextlib import ExitStack
+
+import concourse.mybir as mybir
+
+K, T, E, C, N, M = 2560, 768, 4, 128, 512, 512
+
+FLOPS = 2 * E * C * K * N + 2 * E * C * N * M
+
+F32 = mybir.dt.float32
+BF16 = mybir.dt.bfloat16
+U32 = mybir.dt.uint32
+I32 = mybir.dt.int32
+U16 = mybir.dt.uint16
+U8 = mybir.dt.uint8
+FP8X4 = mybir.dt.float8_e4m3fn_x4
+
+MULT = mybir.AluOpType.mult
+IDENTITY = mybir.ActivationFunctionType.Identity
+
+P = 128
+PACK = 4
+K_PASS = P * PACK
+PASSES = K // K_PASS
+SLOTS = E * C
+TOKENS_A = 512
+LOOKAHEAD = 8
+
+
+def tile_moe_nxt_lin_bias_kernel(tc, xT, w, b, wp, gate, offs, out):
+    nc = tc.nc
+    w_rows = w.rearrange("e k n -> (e k) n")
+
+    with ExitStack() as ctx:
+        held = ctx.enter_context(tc.tile_pool(name="held", bufs=1))
+        w_in = ctx.enter_context(tc.tile_pool(name="w_in", bufs=LOOKAHEAD))
+        mid = ctx.enter_context(tc.tile_pool(name="mid", bufs=2))
+        w_mid = ctx.enter_context(tc.tile_pool(name="w_mid", bufs=3))
+        w_q = ctx.enter_context(tc.tile_pool(name="w_q", bufs=4))
+        acc_pool = ctx.enter_context(tc.psum_pool(name="acc_pool", bufs=6))
+        proj_pool = ctx.enter_context(tc.psum_pool(name="proj_pool", bufs=2))
+
+        offsets = held.tile([P, SLOTS // 16], U16, name="offsets")
+        nc.sync.dma_start(offsets[:], offs)
+
+        gate_sb = held.tile([P, SLOTS], F32, name="gate_sb")
+        bias_sb = held.tile([P, PACK, E], F32, name="bias_sb")
+
+        x_codes = [held.tile([P, T], U32, name=f"x_codes{a}", align_bytes=64) for a in range(PASSES)]
+        x_planes = [held.tile([P, T], U8, name=f"x_planes{i}", align_bytes=64) for i in range(2)]
+        s_codes = [held.tile([P, SLOTS], U32, name=f"s_codes{a}", align_bytes=64) for a in range(PASSES)]
+        s_planes = [held.tile([P, SLOTS], U8, name=f"s_planes{i}", align_bytes=64) for i in range(2)]
+        wp_codes = held.tile([P, M], U32, name="wp_codes", align_bytes=64)
+        wp_scales = held.tile([P, M], U8, name="wp_scales", align_bytes=64)
+        out_sb = [held.tile([P, T], F32, name=f"out_sb{f}") for f in range(M // P)]
+        x_raw = [held.tile([P, PACK, T], F32, name=f"x_raw{a}") for a in range(PASSES)]
+        wp_raw = held.tile([P, PACK, M], F32, name="wp_raw")
+
+        for plane in x_planes:
+            nc.gpsimd.memset(plane[:], 0)
+        for f in range(M // P):
+            nc.gpsimd.memset(out_sb[f][:], 0.0)
+
+        units = [("x", a) for a in range(PASSES)] + [("w", u) for u in range(E * PASSES)]
+        units.insert(PASSES + 3, ("p", 0))
+        last = ("w", E * PASSES - 1)
+        w_raw, w_half, w_code, acc = {}, {}, {}, {}
+
+        def load(unit):
+            kind, i = unit
+            if kind == "x":
+                src = xT[i * K_PASS : (i + 1) * K_PASS, :].rearrange("(p j) t -> p j t", j=PACK)
+                if i == 0:
+                    for lo, hi in ((0, 256), (256, T)):
+                        nc.sync.dma_start(x_raw[0][:, :, lo:hi], src[:, :, lo:hi])
+                    nc.sync.dma_start(bias_sb[:], b.rearrange("(p t) e -> p t e", t=PACK))
+                else:
+                    nc.sync.dma_start(x_raw[i][:], src)
+            elif kind == "p":
+                nc.sync.dma_start(wp_raw[:], wp.rearrange("(p j) f -> p j f", j=PACK))
+                nc.sync.dma_start(gate_sb[:], gate[0:P, :])
+            else:
+                raw = w_in.tile([P, PACK, N], F32, name="raw")
+                src = w_rows[i * K_PASS : (i + 1) * K_PASS, :].rearrange("(p j) n -> p j n", j=PACK)
+                if unit == last:
+                    for h in range(2):
+                        nc.sync.dma_start(raw[:, :, 256 * h : 256 * h + 256], src[:, :, 256 * h : 256 * h + 256])
+                else:
+                    nc.sync.dma_start(raw[:], src)
+                w_raw[i] = raw
+
+        def copy(unit):
+            kind, i = unit
+            if kind == "x":
+                ga = mid.tile([P, TOKENS_A, PACK], BF16, name="ga", align_bytes=64)
+                gb = mid.tile([P, T - TOKENS_A, PACK], BF16, name="gb", align_bytes=64)
+                parts = [(ga, 0, TOKENS_A, "s"), (gb, TOKENS_A, T, "v" if i in (0, 3) else "s")]
+                for tile, lo, hi, eng in parts:
+                    dst = tile[:].rearrange("p (c i) j -> p c j i", i=4)
+                    src = x_raw[i][:, :, lo:hi].rearrange("p j (c i) -> p c j i", i=4)
+                    if eng == "s":
+                        nc.scalar.copy(dst, src)
+                    else:
+                        nc.vector.tensor_copy(dst, src)
+                w_half[unit] = (ga, gb)
+            else:
+                g = w_mid.tile([P, N, PACK], BF16, name="g", align_bytes=64)
+                w_half[unit] = (g,)
+                if kind == "p":
+                    for lo, hi, eng in ((0, 256, "v"), (256, 512, "s")):
+                        dst = g[:, lo:hi, :].rearrange("p (c i) j -> p c j i", i=4)
+                        src = wp_raw[:, :, lo:hi].rearrange("p j (c i) -> p c j i", i=4)
+                        if eng == "v":
+                            nc.vector.tensor_copy(dst, src)
+                        else:
+                            nc.scalar.copy(dst, src)
+                else:
+                    cuts = ((0, 64), (64, 128)) if unit == last else ((0, 128),)
+                    split = 2 if unit == last else 1
+                    for lo, hi in cuts:
+                        for t0, t1 in ((0, split), (split, 4)):
+                            dst = g[:, t0 * P : t1 * P, :].rearrange("p (t m) j -> p m j t", m=P)[:, lo:hi, :, :]
+                            src = w_raw[i][:].rearrange("p j (m t) -> p m j t", t=4)[:, lo:hi, :, t0:t1]
+                            if t0 == 0:
+                                nc.vector.tensor_copy(dst, src)
+                            else:
+                                nc.scalar.copy(dst, src)
+
+        def quantize(unit):
+            kind, i = unit
+            tiles = w_half[unit]
+            if kind == "x":
+                codes, scales = x_codes[i], x_planes[i // 4][4 * (i % 4) : P, :]
+                cols = ((0, TOKENS_A, tiles[0][:]), (TOKENS_A, T, tiles[1][:]))
+            elif kind == "p":
+                codes, scales, cols = wp_codes, wp_scales[:], ((0, M, tiles[0][:]),)
+            else:
+                codes = w_q.tile([P, N], U32, name="codes", align_bytes=64)
+                plane = w_q.tile([P, N], U8, name="plane", align_bytes=64)
+                w_code[i] = (codes, plane)
+                scales = plane[:]
+                if unit == last:
+                    cols = ((0, 256, tiles[0][:, 0:256, :]), (256, 512, tiles[0][:, 256:512, :]))
+                else:
+                    cols = ((0, N, tiles[0][:]),)
+            for lo, hi, src in cols:
+                nc.vector.quantize_mx(
+                    out=codes[:, lo:hi].bitcast(FP8X4),
+                    scales=scales[:, lo:hi],
+                    in_=src.rearrange("p c j -> p (c j)"),
+                )
+
+        def use(unit):
+            kind, i = unit
+            if kind == "x":
+                nc.vector.tensor_copy(s_codes[i][:], x_codes[i][:].indirect(offsets[:]))
+                if i == 3 or i == 4:
+                    nc.vector.tensor_copy(s_planes[i // 4][:], x_planes[i // 4][:].indirect(offsets[:]))
+            elif kind == "w":
+                e, a = divmod(i, PASSES)
+                if a == 0:
+                    acc[e] = [acc_pool.tile([P, C], F32, name="acc_t") for t in range(PACK)]
+                codes, scales = w_code[i]
+                slots = slice(e * C, (e + 1) * C)
+                for t in range(PACK):
+                    cols = slice(t * P, (t + 1) * P)
+                    nc.tensor.matmul_mx(
+                        out=acc[e][t][:],
+                        lhsT=codes[:, cols].bitcast(FP8X4),
+                        lhsT_scale=scales[:, cols],
+                        rhs=s_codes[a][:, slots].bitcast(FP8X4),
+                        rhs_scale=s_planes[a // 4][4 * (a % 4) : P, slots],
+                        start=(a == 0),
+                        stop=(a == PASSES - 1),
+                    )
+
+        def finish(e):
+            slots = slice(e * C, (e + 1) * C)
+            y = mid.tile([P, PACK, C], F32, name="y")
+            c_grouped = mid.tile([P, C, PACK], BF16, name="c_grouped", align_bytes=64)
+            c_codes = mid.tile([P, C], U32, name="c_codes", align_bytes=64)
+            c_scales = mid.tile([P, C], U8, name="c_scales", align_bytes=64)
+            o_sb = mid.tile([P, M // P, C], F32, name="o_sb")
+            proj = proj_pool.tile([P, M // P, C], F32, name="proj")
+
+            def bias():
+                for t in range(PACK):
+                    if e == E - 1 and t % 2 == 1:
+                        nc.vector.tensor_scalar_add(y[:, t, :], acc[e][t][:], bias_sb[:, t, e : e + 1])
+                    else:
+                        nc.scalar.activation(y[:, t, :], acc[e][t][:], IDENTITY, bias=bias_sb[:, t, e : e + 1])
+
+            def gated():
+                nc.vector.tensor_tensor(
+                    c_grouped[:],
+                    y[:].rearrange("p t j -> p j t"),
+                    gate_sb[:, slots].unsqueeze(2).to_broadcast([P, C, PACK]),
+                    MULT,
+                )
+
+            def quant():
+                nc.vector.quantize_mx(
+                    out=c_codes[:].bitcast(FP8X4), scales=c_scales[:], in_=c_grouped[:].rearrange("p c j -> p (c j)")
+                )
+
+            def project():
+                for f in range(M // P):
+                    cols = slice(f * P, (f + 1) * P)
+                    nc.tensor.matmul_mx(
+                        out=proj[:, f, :],
+                        lhsT=wp_codes[:, cols].bitcast(FP8X4),
+                        lhsT_scale=wp_scales[:, cols],
+                        rhs=c_codes[:].bitcast(FP8X4),
+                        rhs_scale=c_scales[:],
+                        start=True,
+                        stop=True,
+                    )
+
+            def leave():
+                if e == E - 1:
+                    for f in range(M // P):
+                        nc.scalar.copy(o_sb[:, f, :], proj[:, f, :])
+                else:
+                    nc.scalar.copy(o_sb[:], proj[:])
+
+            def scatter(f):
+                nc.vector.tensor_copy(out_sb[f][:].indirect(offsets[:, e * C // 16 : (e + 1) * C // 16]), o_sb[:, f, :])
+                if e == E - 1:
+                    nc.sync.dma_start(out[f * P : (f + 1) * P, :], out_sb[f][:])
+
+            return [bias, gated, quant, project, leave] + [lambda f=f: scatter(f) for f in range(M // P)]
+
+        for unit in units[:LOOKAHEAD]:
+            load(unit)
+        tasks = []
+        for s in range(len(units) + 2):
+            for _ in range(2):
+                if tasks:
+                    tasks.pop(0)()
+            if s >= 2:
+                use(units[s - 2])
+                kind, i = units[s - 2]
+                if kind == "w" and i % PASSES == PASSES - 1:
+                    tasks.extend(finish(i // PASSES))
+            if 1 <= s <= len(units):
+                quantize(units[s - 1])
+            if s < len(units):
+                copy(units[s])
+            if s + LOOKAHEAD < len(units):
+                load(units[s + LOOKAHEAD])
+        for task in tasks:
+            task()

@@ -24,6 +24,8 @@ PASSES = K // K_PASS
 SLOTS = E * C
 TOKENS_A = 512
 LOOKAHEAD = 8
+X_TAIL = "vvsvv"
+W_SPLIT = (2, 2, 2, 2, 2, 2, 1, 2, 1, 1, 1, 1, 2, 1, 1, 1, 1, 1, 1, 2)
 
 
 def tile_moe_nxt_lin_bias_kernel(tc, xT, w, b, wp, gate, offs, out):
@@ -36,6 +38,7 @@ def tile_moe_nxt_lin_bias_kernel(tc, xT, w, b, wp, gate, offs, out):
         mid = ctx.enter_context(tc.tile_pool(name="mid", bufs=2))
         w_mid = ctx.enter_context(tc.tile_pool(name="w_mid", bufs=3))
         w_q = ctx.enter_context(tc.tile_pool(name="w_q", bufs=4))
+        o_pool = ctx.enter_context(tc.tile_pool(name="o_pool", bufs=4))
         acc_pool = ctx.enter_context(tc.psum_pool(name="acc_pool", bufs=6))
         proj_pool = ctx.enter_context(tc.psum_pool(name="proj_pool", bufs=2))
 
@@ -70,7 +73,7 @@ def tile_moe_nxt_lin_bias_kernel(tc, xT, w, b, wp, gate, offs, out):
             if kind == "x":
                 src = xT[i * K_PASS : (i + 1) * K_PASS, :].rearrange("(p j) t -> p j t", j=PACK)
                 if i == 0:
-                    for lo, hi in ((0, 256), (256, T)):
+                    for lo, hi in ((0, 256), (256, 512), (512, T)):
                         nc.sync.dma_start(x_raw[0][:, :, lo:hi], src[:, :, lo:hi])
                     nc.sync.dma_start(bias_sb[:], b.rearrange("(p t) e -> p t e", t=PACK))
                 else:
@@ -93,9 +96,11 @@ def tile_moe_nxt_lin_bias_kernel(tc, xT, w, b, wp, gate, offs, out):
             if kind == "x":
                 ga = mid.tile([P, TOKENS_A, PACK], BF16, name="ga", align_bytes=64)
                 gb = mid.tile([P, T - TOKENS_A, PACK], BF16, name="gb", align_bytes=64)
-                parts = [(ga, 0, TOKENS_A, "s"), (gb, TOKENS_A, T, "v" if i in (0, 3) else "s")]
+                ga_parts = ((0, 256), (256, TOKENS_A)) if i == 0 else ((0, TOKENS_A),)
+                parts = [(ga[:, lo:hi, :], lo, hi, "v" if i == 0 and lo == 0 else "s") for lo, hi in ga_parts]
+                parts.append((gb[:], TOKENS_A, T, X_TAIL[i]))
                 for tile, lo, hi, eng in parts:
-                    dst = tile[:].rearrange("p (c i) j -> p c j i", i=4)
+                    dst = tile.rearrange("p (c i) j -> p c j i", i=4)
                     src = x_raw[i][:, :, lo:hi].rearrange("p j (c i) -> p c j i", i=4)
                     if eng == "s":
                         nc.scalar.copy(dst, src)
@@ -115,7 +120,7 @@ def tile_moe_nxt_lin_bias_kernel(tc, xT, w, b, wp, gate, offs, out):
                             nc.scalar.copy(dst, src)
                 else:
                     cuts = ((0, 64), (64, 128)) if unit == last else ((0, 128),)
-                    split = 2 if unit == last else 1
+                    split = W_SPLIT[i]
                     for lo, hi in cuts:
                         for t0, t1 in ((0, split), (split, 4)):
                             dst = g[:, t0 * P : t1 * P, :].rearrange("p (t m) j -> p m j t", m=P)[:, lo:hi, :, :]
@@ -179,7 +184,7 @@ def tile_moe_nxt_lin_bias_kernel(tc, xT, w, b, wp, gate, offs, out):
             c_grouped = mid.tile([P, C, PACK], BF16, name="c_grouped", align_bytes=64)
             c_codes = mid.tile([P, C], U32, name="c_codes", align_bytes=64)
             c_scales = mid.tile([P, C], U8, name="c_scales", align_bytes=64)
-            o_sb = mid.tile([P, M // P, C], F32, name="o_sb")
+            o_sb = o_pool.tile([P, M // P, C], F32, name="o_sb")
             proj = proj_pool.tile([P, M // P, C], F32, name="proj")
 
             def bias():
@@ -227,25 +232,37 @@ def tile_moe_nxt_lin_bias_kernel(tc, xT, w, b, wp, gate, offs, out):
                 if e == E - 1:
                     nc.sync.dma_start(out[f * P : (f + 1) * P, :], out_sb[f][:])
 
-            return [bias, gated, quant, project, leave] + [lambda f=f: scatter(f) for f in range(M // P)]
+            return bias, gated, quant, project, leave, scatter
 
         for unit in units[:LOOKAHEAD]:
             load(unit)
-        tasks = []
-        for s in range(len(units) + 2):
-            for _ in range(2):
-                if tasks:
-                    tasks.pop(0)()
-            if s >= 2:
+        pending, scatters = [], []
+        for s in range(len(units) + 1):
+            if pending:
+                pending.pop(0)()
+            if scatters and s < len(units) - 1:
+                scatters.pop(0)()
+            if s >= 2 and units[s - 2][0] == "x":
                 use(units[s - 2])
-                kind, i = units[s - 2]
-                if kind == "w" and i % PASSES == PASSES - 1:
-                    tasks.extend(finish(i // PASSES))
-            if 1 <= s <= len(units):
+            if s >= 1:
+                kind, i = units[s - 1]
                 quantize(units[s - 1])
+                if kind == "w":
+                    use(units[s - 1])
+                    if pending:
+                        pending.pop(0)()
+                    if i % PASSES == PASSES - 1:
+                        bias, gated, quant, project, leave, scatter = finish(i // PASSES)
+                        bias()
+                        pending.append(gated)
+                        pending.append(lambda quant=quant, project=project: (quant(), project()))
+                        pending.append(leave)
+                        late = [lambda f=f, scatter=scatter: scatter(f) for f in range(M // P)]
+                        if i // PASSES < E - 1:
+                            pending.append(lambda late=late: scatters.extend(late))
             if s < len(units):
                 copy(units[s])
             if s + LOOKAHEAD < len(units):
                 load(units[s + LOOKAHEAD])
-        for task in tasks:
+        for task in pending[:1] + scatters + pending[1:] + late:
             task()

@@ -25,7 +25,11 @@ SLOTS = E * C
 TOKENS_A = 512
 LOOKAHEAD = 8
 X_TAIL = "vvsvv"
-W_SPLIT = (2, 2, 2, 2, 2, 2, 1, 2, 1, 1, 1, 1, 2, 1, 1, 1, 1, 1, 1, 2)
+WP_AT = 3
+SC_LAG = (2, 3, 4, 0)
+EP_LAG = (0, 1, 0, 0)
+SC_STEP = 1
+W_SPLIT = (2, 2, 2, 2, 2, 2, 2, 0, 0, 2, 0, 2, 0, 0, 2, 2, 2, 2, 0, 2)
 
 
 def tile_moe_nxt_lin_bias_kernel(tc, xT, w, b, wp, gate, offs, out):
@@ -64,7 +68,7 @@ def tile_moe_nxt_lin_bias_kernel(tc, xT, w, b, wp, gate, offs, out):
             nc.gpsimd.memset(out_sb[f][:], 0.0)
 
         units = [("x", a) for a in range(PASSES)] + [("w", u) for u in range(E * PASSES)]
-        units.insert(PASSES + 3, ("p", 0))
+        units.insert(PASSES + WP_AT, ("p", 0))
         last = ("w", E * PASSES - 1)
         w_raw, w_half, w_code, acc = {}, {}, {}, {}
 
@@ -122,10 +126,10 @@ def tile_moe_nxt_lin_bias_kernel(tc, xT, w, b, wp, gate, offs, out):
                     cuts = ((0, 64), (64, 128)) if unit == last else ((0, 128),)
                     split = W_SPLIT[i]
                     for lo, hi in cuts:
-                        for t0, t1 in ((0, split), (split, 4)):
+                        for t0, t1 in ((0, 2), (2, 4)):
                             dst = g[:, t0 * P : t1 * P, :].rearrange("p (t m) j -> p m j t", m=P)[:, lo:hi, :, :]
                             src = w_raw[i][:].rearrange("p j (m t) -> p m j t", t=4)[:, lo:hi, :, t0:t1]
-                            if t0 == 0:
+                            if t1 <= split:
                                 nc.vector.tensor_copy(dst, src)
                             else:
                                 nc.scalar.copy(dst, src)
@@ -236,12 +240,10 @@ def tile_moe_nxt_lin_bias_kernel(tc, xT, w, b, wp, gate, offs, out):
 
         for unit in units[:LOOKAHEAD]:
             load(unit)
-        pending, scatters = [], []
+        pending = []
         for s in range(len(units) + 1):
-            if pending:
-                pending.pop(0)()
-            if scatters and s < len(units) - 1:
-                scatters.pop(0)()
+            while pending and pending[0][0] <= s:
+                pending.pop(0)[1]()
             if s >= 2 and units[s - 2][0] == "x":
                 use(units[s - 2])
             if s >= 1:
@@ -249,20 +251,16 @@ def tile_moe_nxt_lin_bias_kernel(tc, xT, w, b, wp, gate, offs, out):
                 quantize(units[s - 1])
                 if kind == "w":
                     use(units[s - 1])
-                    if pending:
-                        pending.pop(0)()
                     if i % PASSES == PASSES - 1:
                         bias, gated, quant, project, leave, scatter = finish(i // PASSES)
                         bias()
-                        pending.append(gated)
-                        pending.append(lambda quant=quant, project=project: (quant(), project()))
-                        pending.append(leave)
-                        late = [lambda f=f, scatter=scatter: scatter(f) for f in range(M // P)]
-                        if i // PASSES < E - 1:
-                            pending.append(lambda late=late: scatters.extend(late))
+                        e = i // PASSES
+                        pending += [(s + EP_LAG[e], step) for step in (gated, quant, project, leave)]
+                        pending += [(s + SC_LAG[e] + f // SC_STEP, lambda f=f, scatter=scatter: scatter(f)) for f in range(M // P)]
+                        pending = sorted(pending, key=lambda x: x[0])
             if s < len(units):
                 copy(units[s])
             if s + LOOKAHEAD < len(units):
                 load(units[s + LOOKAHEAD])
-        for task in pending[:1] + scatters + pending[1:] + late:
+        for _, task in pending:
             task()

@@ -24,12 +24,29 @@ PASSES = K // K_PASS
 SLOTS = E * C
 TOKENS_A = 512
 LOOKAHEAD = 8
-X_TAIL = "vvsvv"
-WP_AT = 3
-SC_LAG = (2, 3, 4, 0)
-EP_LAG = (0, 1, 0, 0)
-SC_STEP = 1
-W_SPLIT = (2, 2, 2, 2, 2, 2, 2, 0, 0, 2, 0, 2, 0, 0, 2, 2, 2, 2, 0, 2)
+X_BUFS = 3
+G_BUFS = 6
+Q_BUFS = 5
+X_TAIL = "svsvs"
+GROUP_START = {0: 1, 1: 1, 2: 1, 3: 1, 4: 1}
+GROUP_END = {0: 1, 1: 1, 2: 1, 3: 1, 4: 1}
+SHARES = {
+    0: ((0, 128, "s", 0, 4),),
+    1: ((0, 64, "s", 0, 4), (64, 128, "s", 0, 4)),
+    2: ((0, 128, "v", 0, 2), (0, 128, "s", 2, 4)),
+    3: ((0, 32, "s", 0, 4), (32, 64, "s", 0, 4), (64, 96, "s", 0, 4), (96, 128, "s", 0, 4)),
+    4: ((0, 128, "v", 0, 4),),
+    5: ((0, 128, "v", 0, 2), (0, 64, "s", 2, 4), (64, 128, "s", 2, 4)),
+    6: ((0, 64, "v", 0, 4), (64, 96, "s", 0, 4), (96, 128, "s", 0, 4)),
+    7: ((0, 32, "v", 0, 4), (32, 64, "s", 0, 4), (64, 96, "s", 0, 4), (96, 128, "s", 0, 4)),
+}
+LAST_SHARES = ((0, 64, "s", 0, 4), (64, 128, "v", 0, 2), (64, 128, "s", 2, 4))
+WP_COPY = ((0, 512, "v"),)
+WP_AT = 2
+SC_LAG = (2, 2, 2, 0)
+EP_LAG = (0, 0, 0, 0)
+SC_STEP = 2
+W_SPLIT = (6, 2, 3, 5, 2, 2, 6, 7, 3, 2, 2, 5, 6, 0, 0, 2, 2, 2, 1, 2)
 
 
 def tile_moe_nxt_lin_bias_kernel(tc, xT, w, b, wp, gate, offs, out):
@@ -38,10 +55,11 @@ def tile_moe_nxt_lin_bias_kernel(tc, xT, w, b, wp, gate, offs, out):
 
     with ExitStack() as ctx:
         held = ctx.enter_context(tc.tile_pool(name="held", bufs=1))
+        x_in = ctx.enter_context(tc.tile_pool(name="x_in", bufs=X_BUFS))
         w_in = ctx.enter_context(tc.tile_pool(name="w_in", bufs=LOOKAHEAD))
         mid = ctx.enter_context(tc.tile_pool(name="mid", bufs=2))
-        w_mid = ctx.enter_context(tc.tile_pool(name="w_mid", bufs=3))
-        w_q = ctx.enter_context(tc.tile_pool(name="w_q", bufs=4))
+        w_mid = ctx.enter_context(tc.tile_pool(name="w_mid", bufs=G_BUFS))
+        w_q = ctx.enter_context(tc.tile_pool(name="w_q", bufs=Q_BUFS))
         o_pool = ctx.enter_context(tc.tile_pool(name="o_pool", bufs=4))
         acc_pool = ctx.enter_context(tc.psum_pool(name="acc_pool", bufs=6))
         proj_pool = ctx.enter_context(tc.psum_pool(name="proj_pool", bufs=2))
@@ -59,7 +77,7 @@ def tile_moe_nxt_lin_bias_kernel(tc, xT, w, b, wp, gate, offs, out):
         wp_codes = held.tile([P, M], U32, name="wp_codes", align_bytes=64)
         wp_scales = held.tile([P, M], U8, name="wp_scales", align_bytes=64)
         out_sb = [held.tile([P, T], F32, name=f"out_sb{f}") for f in range(M // P)]
-        x_raw = [held.tile([P, PACK, T], F32, name=f"x_raw{a}") for a in range(PASSES)]
+        x_raw = {}
         wp_raw = held.tile([P, PACK, M], F32, name="wp_raw")
 
         for plane in x_planes:
@@ -75,6 +93,7 @@ def tile_moe_nxt_lin_bias_kernel(tc, xT, w, b, wp, gate, offs, out):
         def load(unit):
             kind, i = unit
             if kind == "x":
+                x_raw[i] = x_in.tile([P, PACK, T], F32, name="x_in_tile")
                 src = xT[i * K_PASS : (i + 1) * K_PASS, :].rearrange("(p j) t -> p j t", j=PACK)
                 if i == 0:
                     for lo, hi in ((0, 256), (256, 512), (512, T)):
@@ -101,7 +120,7 @@ def tile_moe_nxt_lin_bias_kernel(tc, xT, w, b, wp, gate, offs, out):
                 ga = mid.tile([P, TOKENS_A, PACK], BF16, name="ga", align_bytes=64)
                 gb = mid.tile([P, T - TOKENS_A, PACK], BF16, name="gb", align_bytes=64)
                 ga_parts = ((0, 256), (256, TOKENS_A)) if i == 0 else ((0, TOKENS_A),)
-                parts = [(ga[:, lo:hi, :], lo, hi, "v" if i == 0 and lo == 0 else "s") for lo, hi in ga_parts]
+                parts = [(ga[:, lo:hi, :], lo, hi, "v" if i == 0 and lo == 0 and X_TAIL[0] == "v" else "s") for lo, hi in ga_parts]
                 parts.append((gb[:], TOKENS_A, T, X_TAIL[i]))
                 for tile, lo, hi, eng in parts:
                     dst = tile.rearrange("p (c i) j -> p c j i", i=4)
@@ -112,10 +131,10 @@ def tile_moe_nxt_lin_bias_kernel(tc, xT, w, b, wp, gate, offs, out):
                         nc.vector.tensor_copy(dst, src)
                 w_half[unit] = (ga, gb)
             else:
-                g = w_mid.tile([P, N, PACK], BF16, name="g", align_bytes=64)
-                w_half[unit] = (g,)
                 if kind == "p":
-                    for lo, hi, eng in ((0, 256, "v"), (256, 512, "s")):
+                    g = mid.tile([P, N, PACK], BF16, name="wpg", align_bytes=64)
+                    w_half[unit] = (g,)
+                    for lo, hi, eng in WP_COPY:
                         dst = g[:, lo:hi, :].rearrange("p (c i) j -> p c j i", i=4)
                         src = wp_raw[:, :, lo:hi].rearrange("p j (c i) -> p c j i", i=4)
                         if eng == "v":
@@ -123,34 +142,44 @@ def tile_moe_nxt_lin_bias_kernel(tc, xT, w, b, wp, gate, offs, out):
                         else:
                             nc.scalar.copy(dst, src)
                 else:
-                    cuts = ((0, 64), (64, 128)) if unit == last else ((0, 128),)
-                    split = W_SPLIT[i]
-                    for lo, hi in cuts:
-                        for t0, t1 in ((0, 2), (2, 4)):
+                    e, a = divmod(i, PASSES)
+                    if a in GROUP_START:
+                        w_half[i] = w_mid.tile([P, GROUP_START[a], N, PACK], BF16, name="g", align_bytes=64)
+                    else:
+                        w_half[i] = w_half[i - 1]
+                    g = w_half[i][:, 0 if a in GROUP_START else 1, :, :]
+                    for lo, hi, eng, t0, t1 in LAST_SHARES if unit == last else SHARES[W_SPLIT[i]]:
+                        if True:
                             dst = g[:, t0 * P : t1 * P, :].rearrange("p (t m) j -> p m j t", m=P)[:, lo:hi, :, :]
                             src = w_raw[i][:].rearrange("p j (m t) -> p m j t", t=4)[:, lo:hi, :, t0:t1]
-                            if t1 <= split:
+                            if eng == "v":
                                 nc.vector.tensor_copy(dst, src)
                             else:
                                 nc.scalar.copy(dst, src)
 
         def quantize(unit):
             kind, i = unit
-            tiles = w_half[unit]
             if kind == "x":
                 codes, scales = x_codes[i], x_planes[i // 4][4 * (i % 4) : P, :]
+                tiles = w_half[unit]
                 cols = ((0, TOKENS_A, tiles[0][:]), (TOKENS_A, T, tiles[1][:]))
             elif kind == "p":
-                codes, scales, cols = wp_codes, wp_scales[:], ((0, M, tiles[0][:]),)
+                codes, scales, cols = wp_codes, wp_scales[:], ((0, M, w_half[unit][0][:]),)
             else:
-                codes = w_q.tile([P, N], U32, name="codes", align_bytes=64)
-                plane = w_q.tile([P, N], U8, name="plane", align_bytes=64)
-                w_code[i] = (codes, plane)
+                a = i % PASSES
+                if a in GROUP_START and GROUP_START[a] == 2:
+                    return
+                n = 1 if a in GROUP_START else 2
+                codes = w_q.tile([P, n * N], U32, name="codes", align_bytes=64)
+                plane = w_q.tile([P, n * N], U8, name="plane", align_bytes=64)
+                w_code[i] = (codes, plane, (n - 1) * N)
+                w_code[i + 1 - n] = (codes, plane, 0)
                 scales = plane[:]
+                g = w_half[i][:].rearrange("p a c j -> p (a c) j")
                 if unit == last:
-                    cols = ((0, 256, tiles[0][:, 0:256, :]), (256, 512, tiles[0][:, 256:512, :]))
+                    cols = ((0, 256, g[:, 0:256, :]), (256, 512, g[:, 256:512, :]))
                 else:
-                    cols = ((0, N, tiles[0][:]),)
+                    cols = ((0, n * N, g),)
             for lo, hi, src in cols:
                 nc.vector.quantize_mx(
                     out=codes[:, lo:hi].bitcast(FP8X4),
@@ -168,10 +197,10 @@ def tile_moe_nxt_lin_bias_kernel(tc, xT, w, b, wp, gate, offs, out):
                 e, a = divmod(i, PASSES)
                 if a == 0:
                     acc[e] = [acc_pool.tile([P, C], F32, name="acc_t") for t in range(PACK)]
-                codes, scales = w_code[i]
+                codes, scales, base = w_code[i]
                 slots = slice(e * C, (e + 1) * C)
                 for t in range(PACK):
-                    cols = slice(t * P, (t + 1) * P)
+                    cols = slice(base + t * P, base + (t + 1) * P)
                     nc.tensor.matmul_mx(
                         out=acc[e][t][:],
                         lhsT=codes[:, cols].bitcast(FP8X4),
@@ -238,8 +267,10 @@ def tile_moe_nxt_lin_bias_kernel(tc, xT, w, b, wp, gate, offs, out):
 
             return bias, gated, quant, project, leave, scatter
 
-        for unit in units[:LOOKAHEAD]:
-            load(unit)
+        loaded = 0
+        while loaded < X_BUFS:
+            load(units[loaded])
+            loaded += 1
         pending = []
         for s in range(len(units) + 1):
             while pending and pending[0][0] <= s:
@@ -249,8 +280,9 @@ def tile_moe_nxt_lin_bias_kernel(tc, xT, w, b, wp, gate, offs, out):
             if s >= 1:
                 kind, i = units[s - 1]
                 quantize(units[s - 1])
-                if kind == "w":
-                    use(units[s - 1])
+                if kind == "w" and i % PASSES in GROUP_END:
+                    for u in range(i + 1 - GROUP_END[i % PASSES], i + 1):
+                        use(("w", u))
                     if i % PASSES == PASSES - 1:
                         bias, gated, quant, project, leave, scatter = finish(i // PASSES)
                         bias()
@@ -260,7 +292,8 @@ def tile_moe_nxt_lin_bias_kernel(tc, xT, w, b, wp, gate, offs, out):
                         pending = sorted(pending, key=lambda x: x[0])
             if s < len(units):
                 copy(units[s])
-            if s + LOOKAHEAD < len(units):
-                load(units[s + LOOKAHEAD])
+            while loaded < len(units) and loaded <= s + (X_BUFS if units[loaded][0] == "x" else LOOKAHEAD):
+                load(units[loaded])
+                loaded += 1
         for _, task in pending:
             task()

from contextlib import ExitStack

import concourse.mybir as mybir

K, T, E, C, N, M = 2560, 768, 4, 128, 512, 512

FLOPS = 2 * E * C * K * N + 2 * E * C * N * M

F32 = mybir.dt.float32
BF16 = mybir.dt.bfloat16
U32 = mybir.dt.uint32
I32 = mybir.dt.int32
U16 = mybir.dt.uint16
U8 = mybir.dt.uint8
FP8X4 = mybir.dt.float8_e4m3fn_x4

MULT = mybir.AluOpType.mult
IDENTITY = mybir.ActivationFunctionType.Identity

P = 128
PACK = 4
K_PASS = P * PACK
PASSES = K // K_PASS
SLOTS = E * C
TOKENS_A = 512
LOOKAHEAD = 8
X_BUFS = 3
G_BUFS = 6
Q_BUFS = 5
X_TAIL = "svsvs"
GROUP_START = {0: 1, 1: 1, 2: 1, 3: 1, 4: 1}
GROUP_END = {0: 1, 1: 1, 2: 1, 3: 1, 4: 1}
SHARES = {
    0: ((0, 128, "s", 0, 4),),
    1: ((0, 64, "s", 0, 4), (64, 128, "s", 0, 4)),
    2: ((0, 128, "v", 0, 2), (0, 128, "s", 2, 4)),
    3: ((0, 32, "s", 0, 4), (32, 64, "s", 0, 4), (64, 96, "s", 0, 4), (96, 128, "s", 0, 4)),
    4: ((0, 128, "v", 0, 4),),
    5: ((0, 128, "v", 0, 2), (0, 64, "s", 2, 4), (64, 128, "s", 2, 4)),
    6: ((0, 64, "v", 0, 4), (64, 96, "s", 0, 4), (96, 128, "s", 0, 4)),
    7: ((0, 32, "v", 0, 4), (32, 64, "s", 0, 4), (64, 96, "s", 0, 4), (96, 128, "s", 0, 4)),
}
LAST_SHARES = ((0, 64, "s", 0, 4), (64, 128, "v", 0, 2), (64, 128, "s", 2, 4))
WP_COPY = ((0, 512, "v"),)
WP_AT = 2
SC_LAG = (2, 2, 2, 0)
EP_LAG = (0, 0, 0, 0)
SC_STEP = 2
W_SPLIT = (6, 2, 3, 5, 2, 2, 6, 7, 3, 2, 2, 5, 6, 0, 0, 2, 2, 2, 1, 2)


def tile_moe_nxt_lin_bias_kernel(tc, xT, w, b, wp, gate, offs, out):
    nc = tc.nc
    w_rows = w.rearrange("e k n -> (e k) n")

    with ExitStack() as ctx:
        held = ctx.enter_context(tc.tile_pool(name="held", bufs=1))
        x_in = ctx.enter_context(tc.tile_pool(name="x_in", bufs=X_BUFS))
        w_in = ctx.enter_context(tc.tile_pool(name="w_in", bufs=LOOKAHEAD))
        mid = ctx.enter_context(tc.tile_pool(name="mid", bufs=2))
        w_mid = ctx.enter_context(tc.tile_pool(name="w_mid", bufs=G_BUFS))
        w_q = ctx.enter_context(tc.tile_pool(name="w_q", bufs=Q_BUFS))
        o_pool = ctx.enter_context(tc.tile_pool(name="o_pool", bufs=4))
        acc_pool = ctx.enter_context(tc.psum_pool(name="acc_pool", bufs=6))
        proj_pool = ctx.enter_context(tc.psum_pool(name="proj_pool", bufs=2))

        offsets = held.tile([P, SLOTS // 16], U16, name="offsets")
        nc.sync.dma_start(offsets[:], offs)

        gate_sb = held.tile([P, SLOTS], F32, name="gate_sb")
        bias_sb = held.tile([P, PACK, E], F32, name="bias_sb")

        x_codes = [held.tile([P, T], U32, name=f"x_codes{a}", align_bytes=64) for a in range(PASSES)]
        x_planes = [held.tile([P, T], U8, name=f"x_planes{i}", align_bytes=64) for i in range(2)]
        s_codes = [held.tile([P, SLOTS], U32, name=f"s_codes{a}", align_bytes=64) for a in range(PASSES)]
        s_planes = [held.tile([P, SLOTS], U8, name=f"s_planes{i}", align_bytes=64) for i in range(2)]
        wp_codes = held.tile([P, M], U32, name="wp_codes", align_bytes=64)
        wp_scales = held.tile([P, M], U8, name="wp_scales", align_bytes=64)
        out_sb = [held.tile([P, T], F32, name=f"out_sb{f}") for f in range(M // P)]
        x_raw = {}
        wp_raw = held.tile([P, PACK, M], F32, name="wp_raw")

        for plane in x_planes:
            nc.gpsimd.memset(plane[:], 0)
        for f in range(M // P):
            nc.gpsimd.memset(out_sb[f][:], 0.0)

        units = [("x", a) for a in range(PASSES)] + [("w", u) for u in range(E * PASSES)]
        units.insert(PASSES + WP_AT, ("p", 0))
        last = ("w", E * PASSES - 1)
        w_raw, w_half, w_code, acc = {}, {}, {}, {}

        def load(unit):
            kind, i = unit
            if kind == "x":
                x_raw[i] = x_in.tile([P, PACK, T], F32, name="x_in_tile")
                src = xT[i * K_PASS : (i + 1) * K_PASS, :].rearrange("(p j) t -> p j t", j=PACK)
                if i == 0:
                    for lo, hi in ((0, 256), (256, 512), (512, T)):
                        nc.sync.dma_start(x_raw[0][:, :, lo:hi], src[:, :, lo:hi])
                    nc.sync.dma_start(bias_sb[:], b.rearrange("(p t) e -> p t e", t=PACK))
                else:
                    nc.sync.dma_start(x_raw[i][:], src)
            elif kind == "p":
                nc.sync.dma_start(wp_raw[:], wp.rearrange("(p j) f -> p j f", j=PACK))
                nc.sync.dma_start(gate_sb[:], gate[0:P, :])
            else:
                raw = w_in.tile([P, PACK, N], F32, name="raw")
                src = w_rows[i * K_PASS : (i + 1) * K_PASS, :].rearrange("(p j) n -> p j n", j=PACK)
                if unit == last:
                    for h in range(2):
                        nc.sync.dma_start(raw[:, :, 256 * h : 256 * h + 256], src[:, :, 256 * h : 256 * h + 256])
                else:
                    nc.sync.dma_start(raw[:], src)
                w_raw[i] = raw

        def copy(unit):
            kind, i = unit
            if kind == "x":
                ga = mid.tile([P, TOKENS_A, PACK], BF16, name="ga", align_bytes=64)
                gb = mid.tile([P, T - TOKENS_A, PACK], BF16, name="gb", align_bytes=64)
                ga_parts = ((0, 256), (256, TOKENS_A)) if i == 0 else ((0, TOKENS_A),)
                parts = [(ga[:, lo:hi, :], lo, hi, "v" if i == 0 and lo == 0 and X_TAIL[0] == "v" else "s") for lo, hi in ga_parts]
                parts.append((gb[:], TOKENS_A, T, X_TAIL[i]))
                for tile, lo, hi, eng in parts:
                    dst = tile.rearrange("p (c i) j -> p c j i", i=4)
                    src = x_raw[i][:, :, lo:hi].rearrange("p j (c i) -> p c j i", i=4)
                    if eng == "s":
                        nc.scalar.copy(dst, src)
                    else:
                        nc.vector.tensor_copy(dst, src)
                w_half[unit] = (ga, gb)
            else:
                if kind == "p":
                    g = mid.tile([P, N, PACK], BF16, name="wpg", align_bytes=64)
                    w_half[unit] = (g,)
                    for lo, hi, eng in WP_COPY:
                        dst = g[:, lo:hi, :].rearrange("p (c i) j -> p c j i", i=4)
                        src = wp_raw[:, :, lo:hi].rearrange("p j (c i) -> p c j i", i=4)
                        if eng == "v":
                            nc.vector.tensor_copy(dst, src)
                        else:
                            nc.scalar.copy(dst, src)
                else:
                    e, a = divmod(i, PASSES)
                    if a in GROUP_START:
                        w_half[i] = w_mid.tile([P, GROUP_START[a], N, PACK], BF16, name="g", align_bytes=64)
                    else:
                        w_half[i] = w_half[i - 1]
                    g = w_half[i][:, 0 if a in GROUP_START else 1, :, :]
                    for lo, hi, eng, t0, t1 in LAST_SHARES if unit == last else SHARES[W_SPLIT[i]]:
                        if True:
                            dst = g[:, t0 * P : t1 * P, :].rearrange("p (t m) j -> p m j t", m=P)[:, lo:hi, :, :]
                            src = w_raw[i][:].rearrange("p j (m t) -> p m j t", t=4)[:, lo:hi, :, t0:t1]
                            if eng == "v":
                                nc.vector.tensor_copy(dst, src)
                            else:
                                nc.scalar.copy(dst, src)

        def quantize(unit):
            kind, i = unit
            if kind == "x":
                codes, scales = x_codes[i], x_planes[i // 4][4 * (i % 4) : P, :]
                tiles = w_half[unit]
                cols = ((0, TOKENS_A, tiles[0][:]), (TOKENS_A, T, tiles[1][:]))
            elif kind == "p":
                codes, scales, cols = wp_codes, wp_scales[:], ((0, M, w_half[unit][0][:]),)
            else:
                a = i % PASSES
                if a in GROUP_START and GROUP_START[a] == 2:
                    return
                n = 1 if a in GROUP_START else 2
                codes = w_q.tile([P, n * N], U32, name="codes", align_bytes=64)
                plane = w_q.tile([P, n * N], U8, name="plane", align_bytes=64)
                w_code[i] = (codes, plane, (n - 1) * N)
                w_code[i + 1 - n] = (codes, plane, 0)
                scales = plane[:]
                g = w_half[i][:].rearrange("p a c j -> p (a c) j")
                if unit == last:
                    cols = ((0, 256, g[:, 0:256, :]), (256, 512, g[:, 256:512, :]))
                else:
                    cols = ((0, n * N, g),)
            for lo, hi, src in cols:
                nc.vector.quantize_mx(
                    out=codes[:, lo:hi].bitcast(FP8X4),
                    scales=scales[:, lo:hi],
                    in_=src.rearrange("p c j -> p (c j)"),
                )

        def use(unit):
            kind, i = unit
            if kind == "x":
                nc.vector.tensor_copy(s_codes[i][:], x_codes[i][:].indirect(offsets[:]))
                if i == 3 or i == 4:
                    nc.vector.tensor_copy(s_planes[i // 4][:], x_planes[i // 4][:].indirect(offsets[:]))
            elif kind == "w":
                e, a = divmod(i, PASSES)
                if a == 0:
                    acc[e] = [acc_pool.tile([P, C], F32, name="acc_t") for t in range(PACK)]
                codes, scales, base = w_code[i]
                slots = slice(e * C, (e + 1) * C)
                for t in range(PACK):
                    cols = slice(base + t * P, base + (t + 1) * P)
                    nc.tensor.matmul_mx(
                        out=acc[e][t][:],
                        lhsT=codes[:, cols].bitcast(FP8X4),
                        lhsT_scale=scales[:, cols],
                        rhs=s_codes[a][:, slots].bitcast(FP8X4),
                        rhs_scale=s_planes[a // 4][4 * (a % 4) : P, slots],
                        start=(a == 0),
                        stop=(a == PASSES - 1),
                    )

        def finish(e):
            slots = slice(e * C, (e + 1) * C)
            y = mid.tile([P, PACK, C], F32, name="y")
            c_grouped = mid.tile([P, C, PACK], BF16, name="c_grouped", align_bytes=64)
            c_codes = mid.tile([P, C], U32, name="c_codes", align_bytes=64)
            c_scales = mid.tile([P, C], U8, name="c_scales", align_bytes=64)
            o_sb = o_pool.tile([P, M // P, C], F32, name="o_sb")
            proj = proj_pool.tile([P, M // P, C], F32, name="proj")

            def bias():
                for t in range(PACK):
                    if e == E - 1 and t % 2 == 1:
                        nc.vector.tensor_scalar_add(y[:, t, :], acc[e][t][:], bias_sb[:, t, e : e + 1])
                    else:
                        nc.scalar.activation(y[:, t, :], acc[e][t][:], IDENTITY, bias=bias_sb[:, t, e : e + 1])

            def gated():
                nc.vector.tensor_tensor(
                    c_grouped[:],
                    y[:].rearrange("p t j -> p j t"),
                    gate_sb[:, slots].unsqueeze(2).to_broadcast([P, C, PACK]),
                    MULT,
                )

            def quant():
                nc.vector.quantize_mx(
                    out=c_codes[:].bitcast(FP8X4), scales=c_scales[:], in_=c_grouped[:].rearrange("p c j -> p (c j)")
                )

            def project():
                for f in range(M // P):
                    cols = slice(f * P, (f + 1) * P)
                    nc.tensor.matmul_mx(
                        out=proj[:, f, :],
                        lhsT=wp_codes[:, cols].bitcast(FP8X4),
                        lhsT_scale=wp_scales[:, cols],
                        rhs=c_codes[:].bitcast(FP8X4),
                        rhs_scale=c_scales[:],
                        start=True,
                        stop=True,
                    )

            def leave():
                if e == E - 1:
                    for f in range(M // P):
                        nc.scalar.copy(o_sb[:, f, :], proj[:, f, :])
                else:
                    nc.scalar.copy(o_sb[:], proj[:])

            def scatter(f):
                nc.vector.tensor_copy(out_sb[f][:].indirect(offsets[:, e * C // 16 : (e + 1) * C // 16]), o_sb[:, f, :])
                if e == E - 1:
                    nc.sync.dma_start(out[f * P : (f + 1) * P, :], out_sb[f][:])

            return bias, gated, quant, project, leave, scatter

        loaded = 0
        while loaded < X_BUFS:
            load(units[loaded])
            loaded += 1
        pending = []
        for s in range(len(units) + 1):
            while pending and pending[0][0] <= s:
                pending.pop(0)[1]()
            if s >= 2 and units[s - 2][0] == "x":
                use(units[s - 2])
            if s >= 1:
                kind, i = units[s - 1]
                quantize(units[s - 1])
                if kind == "w" and i % PASSES in GROUP_END:
                    for u in range(i + 1 - GROUP_END[i % PASSES], i + 1):
                        use(("w", u))
                    if i % PASSES == PASSES - 1:
                        bias, gated, quant, project, leave, scatter = finish(i // PASSES)
                        bias()
                        e = i // PASSES
                        pending += [(s + EP_LAG[e], step) for step in (gated, quant, project, leave)]
                        pending += [(s + SC_LAG[e] + f // SC_STEP, lambda f=f, scatter=scatter: scatter(f)) for f in range(M // P)]
                        pending = sorted(pending, key=lambda x: x[0])
            if s < len(units):
                copy(units[s])
            while loaded < len(units) and loaded <= s + (X_BUFS if units[loaded][0] == "x" else LOOKAHEAD):
                load(units[loaded])
                loaded += 1
        for _, task in pending:
            task()
